import numpy as np
import ml_dtypes


def mxq(x, axis, fmt="e4m3"):
    dtype, down = {"e4m3": (ml_dtypes.float8_e4m3fn, 7), "e5m2": (ml_dtypes.float8_e5m2, 14)}[fmt]
    v = np.moveaxis(np.asarray(x, np.float32).astype(ml_dtypes.bfloat16).astype(np.float64), axis, -1)
    blocks = v.reshape(v.shape[:-1] + (-1, 32))
    amax = np.abs(blocks).max(-1, keepdims=True)
    byte = np.maximum(np.where(amax > 0, np.frexp(amax)[1] - 1 + 127, 0) - down, 1)
    scale = np.exp2(byte - 127.0)
    codes = (blocks / scale).astype(np.float32).astype(dtype).astype(np.float64)
    return np.moveaxis((codes * scale).reshape(v.shape), -1, axis)


WIDE = False


def mx_kscale(k):
    if not WIDE:
        return np.ones(k)
    levels = np.array([10, -10, 5, -5, 0])
    if k % 512:
        return np.exp2(np.random.permutation(np.resize(levels, k // 32))).repeat(32)
    a = np.empty((k // 512, 16))
    for p in range(k // 512):
        a[p, :8] = np.random.permutation(np.resize(levels, 8))
        for g in range(8):
            far = levels[np.abs(levels - a[p, g]) >= 10]
            a[p, g + 8] = far[np.random.randint(len(far))]
    return np.exp2(a.ravel()).repeat(32)


BF16 = ml_dtypes.bfloat16


def bf(x):
    return np.asarray(x, np.float32).astype(BF16)


def f64(x):
    return np.asarray(x).astype(np.float64)

def planes(Y):
    n, m = Y.shape
    b = f64(bf(Y)).reshape(n // 32, 32, m)
    amax = np.abs(b).max(1)
    byte = np.clip(np.where(amax > 0, np.frexp(amax)[1] - 1 + 127 - 7, 1), 1, 254)
    codes = (b * np.exp2(127.0 - byte)[:, None, :]).reshape(n, m).astype(np.float32).astype(ml_dtypes.float8_e4m3fn).view(np.uint8)
    words = codes.reshape(n // 512, 128, 4, m).transpose(0, 1, 3, 2)
    return np.ascontiguousarray(words), np.ascontiguousarray(byte.astype(np.uint8).reshape(n // 512, 16, m))


C, K, F, U = 2048, 512, 1024, 1536


def setup_inputs():
    s = mx_kscale(K)
    t = mx_kscale(C)
    size = np.exp(0.8 * np.random.randn(U, 1))
    soil_states = np.random.randn(C, K) * s[None, :]
    feature_weights = np.random.randn(K, F) / np.sqrt(K) / s[:, None]
    cell_scale = np.exp(0.3 * np.random.randn(C)) * t
    et_weights = size * np.random.randn(U, C) / np.sqrt(C) / t[None, :]
    et_offset = size[:, 0] * 0.3 * np.random.randn(U)
    et_cap = size * (0.3 + 1.5 * np.abs(np.random.randn(U, F)))
    return {"soil_states": bf(soil_states), "feature_weights": bf(feature_weights),
            "cell_scale": bf(cell_scale), "et_weights": bf(et_weights),
            "et_offset": bf(et_offset), "et_cap": bf(et_cap)}


def reference(soil_states, feature_weights, cell_scale, et_weights, et_offset, et_cap):
    Z = mxq(f64(soil_states), 1, "e4m3") @ mxq(f64(feature_weights), 0, "e4m3")
    G = (np.maximum(Z, 0.0) + np.log(1.0 + np.exp(-np.abs(Z)))) * f64(cell_scale)[:, None]
    R = mxq(f64(et_weights), 1, "e4m3") @ mxq(G, 0, "e4m3")
    y = np.minimum(R + f64(et_offset)[:, None], f64(et_cap))
    Y = y.reshape(U, F)
    words, scales = planes(Y)
    return y, words, scales

@@ -1,0 +1,389 @@
+from contextlib import ExitStack
+
+import concourse.mybir as mybir
+from concourse.masks import make_identity
+
+C, K, F, U = 2048, 512, 1024, 1536
+FLOPS = 2 * C * K * F + 2 * U * C * F
+
+F32 = mybir.dt.float32
+BF16 = mybir.dt.bfloat16
+I32 = mybir.dt.int32
+U32 = mybir.dt.uint32
+U8 = mybir.dt.uint8
+FP8X4 = mybir.dt.float8_e4m3fn_x4
+ALU = mybir.AluOpType
+ACT = mybir.ActivationFunctionType
+
+P = 128
+PACK = 4
+PASS = P * PACK
+BANK = 512
+CELL_GROUPS = C // PASS
+UNIT_GROUPS = U // PASS
+QUARTER = 256
+LINEAR_FROM = 20.0
+LN_FLOOR = 2.0 ** -60
+BANKS_AHEAD = 6
+SPANS = [(0, 256), (256, 256), (512, 256), (768, 256)]
+
+
+def weave(first, second):
+    keyed = [((i + 0.5) / len(first), 0, i, job) for i, job in enumerate(first)]
+    keyed = keyed + [((i + 0.5) / len(second), 1, i, job) for i, job in enumerate(second)]
+    return [entry[3] for entry in sorted(keyed, key=lambda entry: entry[:3])]
+
+
+def tile_capped_evapotranspiration_planes_h3_kernel(
+    tc, soil_states, feature_weights, cell_scale, et_weights, et_offset, et_cap, out_0, out_1, out_2
+):
+    nc = tc.nc
+    with ExitStack() as ctx:
+        keep = ctx.enter_context(tc.tile_pool(name="keep", bufs=1))
+        ring = ctx.enter_context(tc.tile_pool(name="ring", bufs=1))
+        psum = ctx.enter_context(tc.psum_pool(name="psum", bufs=8))
+        ctx.enter_context(tc.manual_schedule())
+
+        def kept(name, shape, dtype):
+            return keep.tile(shape, dtype, name=name, align_bytes=64)
+
+        def ringed(tag, bufs, shape, dtype):
+            return ring.tile(shape, dtype, name=tag, tag=tag, bufs=bufs, align_bytes=64)
+
+        def mx_operand(name, width):
+            return kept(name + "_codes", [P, width], U32), kept(name + "_scales", [P, width], U8)
+
+        def quantize(codes, scales, staged):
+            nc.vector.quantize_mx(out=codes.bitcast(FP8X4), scales=scales, in_=staged)
+
+        def matmul(out, stationary, m_cols, moving, n_cols, start, stop):
+            nc.tensor.matmul_mx(
+                out=out,
+                lhsT=stationary[0][:, m_cols].bitcast(FP8X4),
+                lhsT_scale=stationary[1][:, m_cols],
+                rhs=moving[0][:, n_cols].bitcast(FP8X4),
+                rhs_scale=moving[1][:, n_cols],
+                start=start,
+                stop=stop,
+            )
+
+        identity = kept("identity", [P, P], F32)
+        make_identity(nc, identity[:])
+
+        raw = {}
+
+        def load_rows(name, source):
+            raw[name] = ringed("raw", 12, list(source.shape), BF16)
+            nc.sync.dma_start(out=raw[name][:], in_=source)
+
+        s_rows = soil_states.rearrange("(g m t) k -> g m (t k)", m=P, t=PACK)
+        w_rows = feature_weights.rearrange("(p j) n -> p j n", j=PACK)
+        p_rows = et_weights.rearrange("(g m t) c -> g t m c", m=P, t=PACK)
+        cap_rows = et_cap.rearrange("(g m t) n -> g m t n", m=P, t=PACK)
+        y_rows = out_0.rearrange("(g m t) n -> g m t n", m=P, t=PACK)
+        words_out = out_1.rearrange("g p n t -> g p (n t)").bitcast(I32)
+        scales_out = out_2.bitcast(I32)
+
+        def load_w(q):
+            load_rows(("w", q), w_rows[:, :, q * QUARTER : (q + 1) * QUARTER])
+
+        def load_p(i):
+            load_rows(("p", i), p_rows[i // PACK, i % PACK])
+
+        load_rows(("s", 0), s_rows[0])
+        load_w(0)
+        load_w(1)
+        load_rows(("s", 1), s_rows[1])
+        load_rows(("s", 2), s_rows[2])
+        load_w(2)
+        load_rows(("s", 3), s_rows[3])
+        load_w(3)
+        load_p(0)
+        load_p(1)
+        scale_raw = kept("scale_raw", [P, CELL_GROUPS, PACK], BF16)
+        nc.sync.dma_start(out=scale_raw[:], in_=cell_scale.rearrange("(g p t) -> p g t", p=P, t=PACK))
+        load_p(2)
+        load_p(3)
+        offset = kept("offset", [P, UNIT_GROUPS, PACK], BF16)
+        nc.sync.dma_start(out=offset[:], in_=et_offset.rearrange("(g p t) -> p g t", p=P, t=PACK))
+        cap = [kept("cap%d" % g, [P, PACK, F], BF16) for g in range(UNIT_GROUPS)]
+
+        def load_cap(g):
+            nc.sync.dma_start(out=cap[g][:], in_=cap_rows[g])
+
+        s_mx = [mx_operand("s%d" % g, PASS) for g in range(CELL_GROUPS)]
+        w_mx = [mx_operand("w%d" % q, QUARTER) for q in range(F // QUARTER)]
+        p_mx = [mx_operand("p%d" % i, PASS) for i in range(U // P)]
+        g_mx = {(g, s): mx_operand("g%d_%d" % (g, s), SPANS[s][1]) for g in range(CELL_GROUPS) for s in range(len(SPANS))}
+        y_scales = [kept("y_scales%d" % g, [P, F], U8) for g in range(UNIT_GROUPS)]
+        neg_scale = kept("neg_scale", [P, CELL_GROUPS, PACK], F32)
+
+        live = {}
+
+        def plain(work, gives=None):
+            return (None, work, gives)
+
+        def staged_tile(key):
+            if key not in live:
+                live[key] = ringed("staged", 5, [P, 2048], BF16)
+            return live[key]
+
+        def turn_jobs(name, engines):
+            jobs = []
+            for half in range(2):
+
+                def fill(bank, half=half):
+                    words = raw[name][:].bitcast(F32)
+                    for seg in range(2):
+                        base = 256 * (2 * half + seg)
+                        for u in range(2):
+                            col = (2 * seg + u) * P
+                            nc.tensor.transpose(bank[:, col : col + P], words[:, base + u : base + 256 : 2], identity[:])
+
+                def work(bank, half=half):
+                    target = staged_tile(name)[:].bitcast(F32)[:, half * BANK : (half + 1) * BANK]
+                    target = target.rearrange("p (s m u) -> p s m u", s=2, u=2)
+                    source = bank[:].rearrange("p (s u m) -> p s m u", s=2, u=2)
+                    if engines[half] == "scalar":
+                        nc.scalar.copy(out=target, in_=source)
+                    else:
+                        nc.vector.tensor_copy(out=target, in_=source)
+
+                jobs.append(([([("loaded", name)], fill)], work, None))
+            return jobs
+
+        def quantize_turned(name, operand):
+            return plain(lambda: quantize(operand[0][:], operand[1][:], live[name][:]), name)
+
+        def w_group(q):
+            def work():
+                target = staged_tile(("w", q))[:, : PACK * QUARTER].rearrange("p (c i j) -> p c j i", i=4, j=PACK)
+                source = raw[("w", q)][:].rearrange("p j (c i) -> p c j i", i=4)
+                nc.vector.tensor_scalar(out=target, in0=source, scalar1=-1.0, scalar2=None, op0=ALU.mult)
+
+            return plain(work)
+
+        def w_quantize(q):
+            return plain(lambda: quantize(w_mx[q][0][:], w_mx[q][1][:], live[("w", q)][:, : PACK * QUARTER]), ("w", q))
+
+        def fill_z(g, q, j):
+            def fill(bank):
+                for t in range(PACK):
+                    cols = slice(t * P, (t + 1) * P)
+                    matmul(bank[:, cols], s_mx[g], cols, w_mx[q], slice(j * P, (j + 1) * P), True, True)
+
+            return fill
+
+        def block_of(g, q, j):
+            return live[("soft", g, q)][:, j * BANK : (j + 1) * BANK].rearrange("p (n t) -> p n t", t=PACK)
+
+        def sigmoid_job(g, q, j):
+            def work(bank):
+                if j == 0:
+                    live[("soft", g, q)] = ringed("soft", 12, [P, PACK * QUARTER], F32)
+                nc.scalar.activation(out=block_of(g, q, j), in_=bank[:].rearrange("p (t n) -> p n t", t=PACK), func=ACT.Sigmoid)
+
+            return ([([("s", g), ("w", q)], fill_z(g, q, j))], work, None)
+
+        def ln_job(g, q):
+            def work():
+                soft = live[("soft", g, q)]
+                nc.scalar.activation(out=soft[:], in_=soft[:], func=ACT.Ln, bias=LN_FLOOR)
+
+            return plain(work)
+
+        def linear_job(g, q, j):
+            def work(bank):
+                nc.vector.scalar_tensor_tensor(
+                    out=block_of(g, q, j),
+                    in0=block_of(g, q, j),
+                    scalar=-LINEAR_FROM,
+                    in1=bank[:].rearrange("p (t n) -> p n t", t=PACK),
+                    op0=ALU.max,
+                    op1=ALU.min,
+                )
+
+            return ([([("s", g), ("w", q)], fill_z(g, q, j))], work, None)
+
+        def scale_job(g, q):
+            def work():
+                target = staged_tile(("g", g, q))[:, : PACK * QUARTER].rearrange("p (n t) -> p n t", t=PACK)
+                nc.vector.tensor_tensor(
+                    out=target,
+                    in0=live[("soft", g, q)][:].rearrange("p (n t) -> p n t", t=PACK),
+                    in1=neg_scale[:, g : g + 1, :].to_broadcast([P, QUARTER, PACK]),
+                    op=ALU.mult,
+                )
+
+            return plain(work)
+
+        def g_quantize(g, q):
+            s = max(i for i in range(len(SPANS)) if SPANS[i][0] <= q * QUARTER)
+            first = q * QUARTER - SPANS[s][0]
+            cols = slice(first, first + QUARTER)
+            codes, scales = g_mx[(g, s)]
+            return plain(lambda: quantize(codes[:, cols], scales[:, cols], live[("g", g, q)][:, : PACK * QUARTER]), ("g", g, q))
+
+        def g_chain(units):
+            jobs = []
+            for i, (g, q) in enumerate(units):
+                step = [linear_job(g, q, 0), linear_job(g, q, 1)]
+                if i > 0:
+                    step.append(g_quantize(*units[i - 1]))
+                step.append(scale_job(g, q))
+                jobs.append(step)
+            return jobs
+
+        def cap_job(ug, s, t):
+            first, width = SPANS[s]
+            quarters = range(first // QUARTER, (first + width) // QUARTER)
+
+            def one_pass(g):
+                def fill(bank):
+                    matmul(bank[:, :width], p_mx[PACK * ug + t], slice(g * P, (g + 1) * P), g_mx[(g, s)], slice(0, width), g == 0, g == CELL_GROUPS - 1)
+
+                return ([("p", PACK * ug + t)] + [("g", g, q) for q in quarters], fill)
+
+            def work(bank):
+                if t == 0:
+                    live[("y", ug, s)] = ringed("y", 5, [P, PACK, width], F32)
+                y = live[("y", ug, s)]
+                nc.vector.scalar_tensor_tensor(
+                    out=y[:, t, :],
+                    in0=bank[:, :width],
+                    scalar=offset[:, ug, t : t + 1],
+                    in1=cap[ug][:, t, first : first + width],
+                    op0=ALU.add,
+                    op1=ALU.min,
+                )
+                if t == PACK - 1:
+                    nc.sync.dma_start(out=y_rows[ug][:, :, first : first + width], in_=y[:])
+
+            return ([one_pass(g) for g in range(CELL_GROUPS)], work, None)
+
+        def y_group(ug, s, engine="scalar"):
+            width = SPANS[s][1]
+
+            def work():
+                target = staged_tile(("yb", ug, s))[:, : PACK * width].rearrange("p (c i t) -> p c t i", i=4, t=PACK)
+                source = live[("y", ug, s)][:].rearrange("p t (c i) -> p c t i", i=4)
+                if engine == "scalar":
+                    nc.scalar.copy(out=target, in_=source)
+                else:
+                    nc.vector.tensor_copy(out=target, in_=source)
+
+            return plain(work)
+
+        def y_quantize(ug, s):
+            first, width = SPANS[s]
+
+            def work():
+                codes = ringed("y_codes", 3, [P, width], U32)
+                quantize(codes[:], y_scales[ug][:, first : first + width], live[("yb", ug, s)][:, : PACK * width])
+                nc.sync.dma_start(out=words_out[ug][:, first : first + width], in_=codes[:].bitcast(I32))
+                if s == len(SPANS) - 1:
+                    for quad in range(4):
+                        nc.sync.dma_start(
+                            out=scales_out[ug, 4 * quad : 4 * quad + 4, :],
+                            in_=y_scales[ug][32 * quad : 32 * quad + 4, :].bitcast(I32),
+                        )
+
+            return plain(work)
+
+        def negate_scale():
+            nc.vector.tensor_scalar(out=neg_scale[:], in0=scale_raw[:], scalar1=-1.0, scalar2=None, op0=ALU.mult)
+
+        def flat(steps):
+            return [job for step in steps for job in step]
+
+        def later_loads(names):
+            def work():
+                for name in names:
+                    if name[0] == "p":
+                        load_p(name[1])
+                    else:
+                        load_cap(name[1])
+
+            return (None, work, [("loaded", name) for name in names])
+
+        def p_copies(i, engine):
+            return turn_jobs(("p", i), [engine, engine])
+
+        def p_quantize(i):
+            return quantize_turned(("p", i), p_mx[i])
+
+        def epilogue(ug, s):
+            return [cap_job(ug, s, t) for t in range(PACK)]
+
+        cells = range(CELL_GROUPS)
+
+        def s_copies(g, engines):
+            return turn_jobs(("s", g), engines)
+
+        def s_quantize(g):
+            return quantize_turned(("s", g), s_mx[g])
+
+        def sigmoids(units):
+            return [sigmoid_job(g, q, j) for (g, q) in units for j in range(2)]
+
+        def quarter(q):
+            return [(g, q) for g in cells]
+
+        order = s_copies(0, ["scalar", "vector"])
+        order = order[:1] + [w_group(0)] + order[1:] + [w_quantize(0), s_quantize(0), w_group(1)]
+        order = order + s_copies(1, ["scalar", "vector"]) + [w_quantize(1), s_quantize(1)]
+        order = order + sigmoids([(0, 0)]) + s_copies(2, ["vector", "vector"]) + sigmoids([(0, 1)]) + [w_group(2), s_quantize(2)]
+        order = order + sigmoids([(1, 0)]) + s_copies(3, ["vector", "vector"]) + sigmoids([(1, 1)]) + [w_group(3), s_quantize(3), w_quantize(2), w_quantize(3)]
+        order = order + [later_loads([("p", 4), ("p", 5), ("p", 6), ("p", 7), ("cap", 0)])]
+        order = order + sigmoids([(2, 0), (2, 1)]) + p_copies(0, "vector") + sigmoids([(3, 0)]) + p_copies(1, "vector") + [p_quantize(0)]
+        order = order + sigmoids([(3, 1)]) + p_copies(2, "vector") + [p_quantize(1), plain(negate_scale)] + p_copies(3, "vector") + [p_quantize(2)]
+        order = order + [later_loads([("cap", 1), ("p", 8), ("p", 9), ("p", 10), ("p", 11), ("cap", 2)])]
+        order = order + [ln_job(*unit) for unit in quarter(0) + quarter(1)]
+        chain = g_chain(quarter(0) + quarter(1) + quarter(2) + quarter(3))
+        order = order + chain[0][:2] + [p_quantize(3)] + chain[0][2:] + flat(chain[1:4])
+        sig = sigmoids(quarter(2) + quarter(3))
+        order = order + p_copies(4, "scalar") + chain[4] + [p_quantize(4)] + sig[:4] + p_copies(5, "scalar")
+        order = order + weave(chain[5] + [p_quantize(5)], epilogue(0, 0)) + sig[4:7] + p_copies(6, "scalar") + sig[7:10]
+        order = order + chain[6] + [p_quantize(6)] + p_copies(7, "scalar") + sig[10:13]
+        order = order + chain[7][:2] + [p_quantize(7)] + chain[7][2:] + sig[13:] + epilogue(1, 0)
+        order = order + [chain[8][2]] + epilogue(0, 1) + epilogue(1, 1)
+        chain[8] = chain[8][:2] + chain[8][3:]
+        order = order + [ln_job(*unit) for unit in quarter(2)] + [y_group(0, 0), y_group(1, 0)]
+        order = order + chain[8] + chain[9] + p_copies(8, "scalar") + [y_quantize(0, 0)] + p_copies(9, "scalar")
+        order = order + [ln_job(*unit) for unit in quarter(3)[:2]] + chain[10] + [y_quantize(1, 0), p_quantize(8)] + p_copies(10, "scalar")
+        order = order + [ln_job(*unit) for unit in quarter(3)[2:]] + chain[11] + [p_quantize(9)] + p_copies(11, "scalar") + [y_group(0, 1)]
+        order = order + chain[12] + [p_quantize(10), y_quantize(0, 1), p_quantize(11), y_group(1, 1)]
+        order = order + weave(chain[13], epilogue(0, 2)) + [y_quantize(1, 1), y_group(0, 2)] + epilogue(2, 0) + [y_group(2, 0)]
+        order = order + weave(chain[14], epilogue(1, 2)) + [y_quantize(0, 2), y_group(1, 2)] + epilogue(2, 1) + [y_quantize(2, 0), y_group(2, 1)]
+        order = order + weave(chain[15], epilogue(2, 2)) + [y_quantize(1, 2), y_group(2, 2), g_quantize(3, 3), y_quantize(2, 1)]
+        order = order + epilogue(0, 3) + [y_quantize(2, 2), y_group(0, 3)] + epilogue(1, 3) + [y_quantize(0, 3), y_group(1, 3)]
+        order = order + epilogue(2, 3) + [y_quantize(1, 3), y_group(2, 3, "vector"), y_quantize(2, 3)]
+
+        done = set(("loaded", name) for name in raw)
+        banks = {}
+        waiting = {}
+        opened = 0
+        for i, (passes, work, gives) in enumerate(order):
+            while True:
+                for k in sorted(waiting):
+                    while waiting[k] and all(need in done for need in waiting[k][0][0]):
+                        waiting[k][0][1](banks[k])
+                        waiting[k] = waiting[k][1:]
+                if opened == len(order) or (opened > i and len(banks) >= BANKS_AHEAD):
+                    break
+                ahead = order[opened][0]
+                if ahead is not None:
+                    if not all(need in done for need in ahead[0][0]):
+                        break
+                    banks[opened] = psum.tile([P, BANK], F32, name="bank", tag="bank")
+                    waiting[opened] = list(ahead)
+                opened = opened + 1
+            if passes is None:
+                work()
+            else:
+                assert not waiting.pop(i)
+                work(banks.pop(i))
+            if isinstance(gives, list):
+                done = done | set(gives)
+            elif gives is not None:
+                done.add(gives)

@@ -25,6 +25,7 @@ QUARTER = 256
 LINEAR_FROM = 20.0
 LN_FLOOR = 2.0 ** -60
 BANKS_AHEAD = 6
+HALVED = [(g, q) for q in range(4) for g in range(4) if 4 * q + g not in (0,1,2,3,6,7,8,9,10,11,12,13,14)]
 SPANS = [(0, 256), (256, 256), (512, 256), (768, 256)]
 
 
@@ -115,7 +116,7 @@ def tile_capped_evapotranspiration_planes_h3_kernel(
         w_mx = [mx_operand("w%d" % q, QUARTER) for q in range(F // QUARTER)]
         p_mx = [mx_operand("p%d" % i, PASS) for i in range(U // P)]
         g_mx = {(g, s): mx_operand("g%d_%d" % (g, s), SPANS[s][1]) for g in range(CELL_GROUPS) for s in range(len(SPANS))}
-        y_scales = [kept("y_scales%d" % g, [P, F], U8) for g in range(UNIT_GROUPS)]
+        y_scales = [kept("y_scales%d" % pair, [P, F], U8) for pair in range(2)]
         neg_scale = kept("neg_scale", [P, CELL_GROUPS, PACK], F32)
 
         live = {}
@@ -205,34 +206,52 @@ def tile_capped_evapotranspiration_planes_h3_kernel(
 
             return ([([("s", g), ("w", q)], fill_z(g, q, j))], work, None)
 
-        def scale_job(g, q):
+        def scale_job(g, q, blocks, on_gpsimd):
             def work():
-                target = staged_tile(("g", g, q))[:, : PACK * QUARTER].rearrange("p (n t) -> p n t", t=PACK)
-                nc.vector.tensor_tensor(
-                    out=target,
-                    in0=live[("soft", g, q)][:].rearrange("p (n t) -> p n t", t=PACK),
-                    in1=neg_scale[:, g : g + 1, :].to_broadcast([P, QUARTER, PACK]),
+                width = P * len(blocks)
+                if on_gpsimd:
+                    staged = ringed("gpsimd_staged", 1, [P, PACK * width], BF16)
+                    engine = nc.gpsimd
+                else:
+                    staged = ringed("vector_staged", 2, [P, PACK * width], BF16)
+                    engine = nc.vector
+                live[("g", g, q, blocks)] = staged
+                source = live[("soft", g, q)][:, blocks[0] * BANK : (blocks[-1] + 1) * BANK]
+                engine.tensor_tensor(
+                    out=staged[:].rearrange("p (n t) -> p n t", t=PACK),
+                    in0=source.rearrange("p (n t) -> p n t", t=PACK),
+                    in1=neg_scale[:, g : g + 1, :].to_broadcast([P, width, PACK]),
                     op=ALU.mult,
                 )
 
             return plain(work)
 
-        def g_quantize(g, q):
-            s = max(i for i in range(len(SPANS)) if SPANS[i][0] <= q * QUARTER)
-            first = q * QUARTER - SPANS[s][0]
-            cols = slice(first, first + QUARTER)
-            codes, scales = g_mx[(g, s)]
-            return plain(lambda: quantize(codes[:, cols], scales[:, cols], live[("g", g, q)][:, : PACK * QUARTER]), ("g", g, q))
+        def g_quantize(g, q, blocks):
+            cols = slice(blocks[0] * P, (blocks[-1] + 1) * P)
+            codes, scales = g_mx[(g, q)]
+            gives = [("g", g, q, j) for j in blocks]
+            return plain(lambda: quantize(codes[:, cols], scales[:, cols], live[("g", g, q, blocks)][:]), gives)
 
-        def g_chain(units):
-            jobs = []
-            for i, (g, q) in enumerate(units):
-                step = [linear_job(g, q, 0), linear_job(g, q, 1)]
-                if i > 0:
-                    step.append(g_quantize(*units[i - 1]))
-                step.append(scale_job(g, q))
-                jobs.append(step)
-            return jobs
+        def shares(unit):
+            if unit == (3, 3):
+                return ((), (0, 1))
+            return ((0,), (1,)) if unit in HALVED else ((0, 1), ())
+
+        def finish(unit):
+            on_gpsimd, on_vector = shares(unit)
+            return [g_quantize(*unit, blocks) for blocks in (on_vector, on_gpsimd) if blocks]
+
+        def g_step(previous, unit, psum_work=(), port_work=()):
+            on_gpsimd, on_vector = shares(unit)
+            step = [linear_job(*unit, 1), linear_job(*unit, 0)]
+            if psum_work:
+                step = weave(step, list(psum_work))
+            if on_vector:
+                step = step + [scale_job(*unit, on_vector, False)]
+            step = step + list(port_work)
+            if previous is not None:
+                step = step + finish(previous)
+            return step + ([scale_job(*unit, on_gpsimd, True)] if on_gpsimd else [])
 
         def cap_job(ug, s, t):
             first, width = SPANS[s]
@@ -242,7 +261,7 @@ def tile_capped_evapotranspiration_planes_h3_kernel(
                 def fill(bank):
                     matmul(bank[:, :width], p_mx[PACK * ug + t], slice(g * P, (g + 1) * P), g_mx[(g, s)], slice(0, width), g == 0, g == CELL_GROUPS - 1)
 
-                return ([("p", PACK * ug + t)] + [("g", g, q) for q in quarters], fill)
+                return ([("p", PACK * ug + t)] + [("g", g, q, j) for q in quarters for j in range(2)], fill)
 
             def work(bank):
                 if t == 0:
@@ -279,13 +298,15 @@ def tile_capped_evapotranspiration_planes_h3_kernel(
 
             def work():
                 codes = ringed("y_codes", 3, [P, width], U32)
-                quantize(codes[:], y_scales[ug][:, first : first + width], live[("yb", ug, s)][:, : PACK * width])
+                quantize(codes[:], y_scales[ug // 2][4 * (ug % 2) :, first : first + width], live[("yb", ug, s)][:, : PACK * width])
                 nc.sync.dma_start(out=words_out[ug][:, first : first + width], in_=codes[:].bitcast(I32))
-                if s == len(SPANS) - 1:
+                if s == len(SPANS) - 1 and ug > 0:
+                    groups = slice(0, 2) if ug == 1 else slice(2, 3)
+                    rows = 4 * (groups.stop - groups.start)
                     for quad in range(4):
                         nc.sync.dma_start(
-                            out=scales_out[ug, 4 * quad : 4 * quad + 4, :],
-                            in_=y_scales[ug][32 * quad : 32 * quad + 4, :].bitcast(I32),
+                            out=scales_out[groups, 4 * quad : 4 * quad + 4, :],
+                            in_=y_scales[ug // 2][32 * quad : 32 * quad + rows, :].bitcast(I32),
                         )
 
             return plain(work)
@@ -336,28 +357,28 @@ def tile_capped_evapotranspiration_planes_h3_kernel(
         order = order + sigmoids([(1, 0)]) + s_copies(3, ["vector", "vector"]) + sigmoids([(1, 1)]) + [w_group(3), s_quantize(3), w_quantize(2), w_quantize(3)]
         order = order + [later_loads([("p", 4), ("p", 5), ("p", 6), ("p", 7), ("cap", 0)])]
         order = order + sigmoids([(2, 0), (2, 1)]) + p_copies(0, "vector") + sigmoids([(3, 0)]) + p_copies(1, "vector") + [p_quantize(0)]
-        order = order + sigmoids([(3, 1)]) + p_copies(2, "vector") + [p_quantize(1), plain(negate_scale)] + p_copies(3, "vector") + [p_quantize(2)]
-        order = order + [later_loads([("cap", 1), ("p", 8), ("p", 9), ("p", 10), ("p", 11), ("cap", 2)])]
-        order = order + [ln_job(*unit) for unit in quarter(0) + quarter(1)]
-        chain = g_chain(quarter(0) + quarter(1) + quarter(2) + quarter(3))
-        order = order + chain[0][:2] + [p_quantize(3)] + chain[0][2:] + flat(chain[1:4])
+        order = order + sigmoids([(3, 1)]) + p_copies(2, "vector") + [p_quantize(1), plain(negate_scale), p_quantize(2)]
+        order = order + [later_loads([("p", 8), ("p", 9), ("p", 10), ("p", 11), ("cap", 1), ("cap", 2)])]
+        u = quarter(0) + quarter(1) + quarter(2) + quarter(3)
         sig = sigmoids(quarter(2) + quarter(3))
-        order = order + p_copies(4, "scalar") + chain[4] + [p_quantize(4)] + sig[:4] + p_copies(5, "scalar")
-        order = order + weave(chain[5] + [p_quantize(5)], epilogue(0, 0)) + sig[4:7] + p_copies(6, "scalar") + sig[7:10]
-        order = order + chain[6] + [p_quantize(6)] + p_copies(7, "scalar") + sig[10:13]
-        order = order + chain[7][:2] + [p_quantize(7)] + chain[7][2:] + sig[13:] + epilogue(1, 0)
-        order = order + [chain[8][2]] + epilogue(0, 1) + epilogue(1, 1)
-        chain[8] = chain[8][:2] + chain[8][3:]
-        order = order + [ln_job(*unit) for unit in quarter(2)] + [y_group(0, 0), y_group(1, 0)]
-        order = order + chain[8] + chain[9] + p_copies(8, "scalar") + [y_quantize(0, 0)] + p_copies(9, "scalar")
-        order = order + [ln_job(*unit) for unit in quarter(3)[:2]] + chain[10] + [y_quantize(1, 0), p_quantize(8)] + p_copies(10, "scalar")
-        order = order + [ln_job(*unit) for unit in quarter(3)[2:]] + chain[11] + [p_quantize(9)] + p_copies(11, "scalar") + [y_group(0, 1)]
-        order = order + chain[12] + [p_quantize(10), y_quantize(0, 1), p_quantize(11), y_group(1, 1)]
-        order = order + weave(chain[13], epilogue(0, 2)) + [y_quantize(1, 1), y_group(0, 2)] + epilogue(2, 0) + [y_group(2, 0)]
-        order = order + weave(chain[14], epilogue(1, 2)) + [y_quantize(0, 2), y_group(1, 2)] + epilogue(2, 1) + [y_quantize(2, 0), y_group(2, 1)]
-        order = order + weave(chain[15], epilogue(2, 2)) + [y_quantize(1, 2), y_group(2, 2), g_quantize(3, 3), y_quantize(2, 1)]
-        order = order + epilogue(0, 3) + [y_quantize(2, 2), y_group(0, 3)] + epilogue(1, 3) + [y_quantize(0, 3), y_group(1, 3)]
-        order = order + epilogue(2, 3) + [y_quantize(1, 3), y_group(2, 3, "vector"), y_quantize(2, 3)]
+        order = order + [ln_job(*u[0]), ln_job(*u[1])] + g_step(None, u[0], p_copies(3, "vector"))
+        order = order + p_copies(4, "scalar") + [ln_job(*u[2]), ln_job(*u[3])] + g_step(u[0], u[1], p_copies(5, "vector"), [p_quantize(3), p_quantize(4)])
+        order = order + p_copies(6, "scalar") + [ln_job(*u[4]), ln_job(*u[5])] + g_step(u[1], u[2], p_copies(7, "vector"), [p_quantize(5), p_quantize(6)])
+        order = order + p_copies(8, "scalar") + [ln_job(*u[6]), ln_job(*u[7])] + g_step(u[2], u[3], p_copies(9, "vector"), [p_quantize(7)])
+        order = order + p_copies(10, "scalar") + weave(sig[:7], g_step(u[3], u[4], p_copies(11, "vector"), [p_quantize(8), p_quantize(9)]))
+        order = order + weave(sig[7:12], g_step(u[4], u[5], [], [p_quantize(10)]))
+        order = order + weave(sig[12:], g_step(u[5], u[6], [], [p_quantize(11)]))
+        order = order + g_step(u[6], u[7], epilogue(0, 0))
+        finished = [(ug, s) for s in range(4) for ug in range(UNIT_GROUPS)]
+        order = order + [ln_job(*u[8]), ln_job(*u[9]), y_group(0, 0)]
+        for i in range(8, 16):
+            order = order + g_step(u[i - 1], u[i], epilogue(*finished[i - 7]), [y_quantize(*finished[i - 8])])
+            if i + 2 < 16:
+                order = order + [ln_job(*u[i + 2])]
+            order = order + [y_group(*finished[i - 7])]
+        order = order + finish(u[15])
+        order = order + epilogue(0, 3) + [y_quantize(2, 2), y_group(0, 3)] + epilogue(1, 3) + [y_group(1, 3), y_quantize(0, 3)]
+        order = order + epilogue(2, 3)[:3] + [y_quantize(1, 3)] + epilogue(2, 3)[3:] + [y_group(2, 3, "vector"), y_quantize(2, 3)]
 
         done = set(("loaded", name) for name in raw)
         banks = {}

@@ -19,14 +19,26 @@ P = 128
 PACK = 4
 PASS = P * PACK
 BANK = 512
+ROW_WORDS = PASS // 2
 CELL_GROUPS = C // PASS
 UNIT_GROUPS = U // PASS
+P_TILES = U // P
 QUARTER = 256
+QUARTERS = F // QUARTER
+BLOCKS = QUARTER // P
+LINE = 4
+
 LINEAR_FROM = 20.0
-LN_FLOOR = 2.0 ** -60
+LN_FLOOR = 2.0**-60
+
+PIECES = [(g, q) for q in range(QUARTERS) for g in range(CELL_GROUPS)]
+HALF = len(PIECES) // 2
+
+VECTOR_FEW = 56
+VECTOR_MANY = 160
+BARE_STEPS = (5, 6)
+SIGMOID_CUTS = (0, 7, 12, BLOCKS * HALF)
 BANKS_AHEAD = 6
-HALVED = [(g, q) for q in range(4) for g in range(4) if 4 * q + g not in (0,1,2,3,6,7,8,9,10,11,12,13,14)]
-SPANS = [(0, 256), (256, 256), (512, 256), (768, 256)]
 
 
 def weave(first, second):
@@ -68,14 +80,20 @@ def tile_capped_evapotranspiration_planes_h3_kernel(
                 stop=stop,
             )
 
+        def copy(engine, out, in_):
+            if engine == "scalar":
+                nc.scalar.copy(out=out, in_=in_)
+            else:
+                nc.vector.tensor_copy(out=out, in_=in_)
+
+        def slots_last(ap):
+            return ap.rearrange("p (n t) -> p n t", t=PACK)
+
+        def bank_slots_last(bank):
+            return bank[:].rearrange("p (t n) -> p n t", t=PACK)
+
         identity = kept("identity", [P, P], F32)
         make_identity(nc, identity[:])
-
-        raw = {}
-
-        def load_rows(name, source):
-            raw[name] = ringed("raw", 12, list(source.shape), BF16)
-            nc.sync.dma_start(out=raw[name][:], in_=source)
 
         s_rows = soil_states.rearrange("(g m t) k -> g m (t k)", m=P, t=PACK)
         w_rows = feature_weights.rearrange("(p j) n -> p j n", j=PACK)
@@ -85,19 +103,35 @@ def tile_capped_evapotranspiration_planes_h3_kernel(
         words_out = out_1.rearrange("g p n t -> g p (n t)").bitcast(I32)
         scales_out = out_2.bitcast(I32)
 
+        raw = {}
+        first_halves = []
+
+        def load_raw(name, source):
+            raw[name] = ringed("raw", 11, list(source.shape), BF16)
+            nc.sync.dma_start(out=raw[name][:], in_=source)
+
+        def load_first_half(half):
+            rows = ringed("raw_half", 2, [P, 2 * K], BF16)
+            nc.sync.dma_start(out=rows[:], in_=s_rows[0][:, half * 2 * K : (half + 1) * 2 * K])
+            first_halves.append(rows)
+
+        def load_s(g):
+            load_raw(("s", g), s_rows[g])
+
         def load_w(q):
-            load_rows(("w", q), w_rows[:, :, q * QUARTER : (q + 1) * QUARTER])
+            load_raw(("w", q), w_rows[:, :, q * QUARTER : (q + 1) * QUARTER])
 
         def load_p(i):
-            load_rows(("p", i), p_rows[i // PACK, i % PACK])
+            load_raw(("p", i), p_rows[i // PACK, i % PACK])
 
-        load_rows(("s", 0), s_rows[0])
+        load_first_half(0)
         load_w(0)
+        load_first_half(1)
+        load_s(1)
         load_w(1)
-        load_rows(("s", 1), s_rows[1])
-        load_rows(("s", 2), s_rows[2])
+        load_s(2)
         load_w(2)
-        load_rows(("s", 3), s_rows[3])
+        load_s(3)
         load_w(3)
         load_p(0)
         load_p(1)
@@ -107,294 +141,288 @@ def tile_capped_evapotranspiration_planes_h3_kernel(
         load_p(3)
         offset = kept("offset", [P, UNIT_GROUPS, PACK], BF16)
         nc.sync.dma_start(out=offset[:], in_=et_offset.rearrange("(g p t) -> p g t", p=P, t=PACK))
-        cap = [kept("cap%d" % g, [P, PACK, F], BF16) for g in range(UNIT_GROUPS)]
 
-        def load_cap(g):
-            nc.sync.dma_start(out=cap[g][:], in_=cap_rows[g])
-
+        cap = [kept("cap%d" % ug, [P, PACK, F], BF16) for ug in range(UNIT_GROUPS)]
         s_mx = [mx_operand("s%d" % g, PASS) for g in range(CELL_GROUPS)]
-        w_mx = [mx_operand("w%d" % q, QUARTER) for q in range(F // QUARTER)]
-        p_mx = [mx_operand("p%d" % i, PASS) for i in range(U // P)]
-        g_mx = {(g, s): mx_operand("g%d_%d" % (g, s), SPANS[s][1]) for g in range(CELL_GROUPS) for s in range(len(SPANS))}
+        w_mx = [mx_operand("w%d" % q, QUARTER) for q in range(QUARTERS)]
+        p_mx = [mx_operand("p%d" % i, PASS) for i in range(P_TILES)]
+        g_mx = {(g, q): mx_operand("g%d_%d" % (g, q), QUARTER) for g in range(CELL_GROUPS) for q in range(QUARTERS)}
         y_scales = [kept("y_scales%d" % pair, [P, F], U8) for pair in range(2)]
         neg_scale = kept("neg_scale", [P, CELL_GROUPS, PACK], F32)
+        g_staged = kept("g_staged", [P, PACK * (QUARTER + VECTOR_MANY)], BF16)
 
         live = {}
 
-        def plain(work, gives=None):
-            return (None, work, gives)
+        def plain(work, gives=()):
+            return (None, work, list(gives))
 
         def staged_tile(key):
             if key not in live:
-                live[key] = ringed("staged", 5, [P, 2048], BF16)
+                live[key] = ringed("staged", 5, [P, PACK * PASS], BF16)
             return live[key]
 
-        def turn_jobs(name, engines):
+        def turn(name, engines):
             jobs = []
             for half in range(2):
 
                 def fill(bank, half=half):
-                    words = raw[name][:].bitcast(F32)
-                    for seg in range(2):
-                        base = 256 * (2 * half + seg)
+                    if name == ("s", 0):
+                        words = first_halves[half][:].bitcast(F32)
+                    else:
+                        words = raw[name][:].bitcast(F32)[:, half * BANK : (half + 1) * BANK]
+                    for part in range(2):
                         for u in range(2):
-                            col = (2 * seg + u) * P
-                            nc.tensor.transpose(bank[:, col : col + P], words[:, base + u : base + 256 : 2], identity[:])
+                            col = (2 * part + u) * P
+                            source = words[:, part * ROW_WORDS + u : (part + 1) * ROW_WORDS : 2]
+                            nc.tensor.transpose(bank[:, col : col + P], source, identity[:])
 
                 def work(bank, half=half):
                     target = staged_tile(name)[:].bitcast(F32)[:, half * BANK : (half + 1) * BANK]
-                    target = target.rearrange("p (s m u) -> p s m u", s=2, u=2)
-                    source = bank[:].rearrange("p (s u m) -> p s m u", s=2, u=2)
-                    if engines[half] == "scalar":
-                        nc.scalar.copy(out=target, in_=source)
-                    else:
-                        nc.vector.tensor_copy(out=target, in_=source)
+                    copy(
+                        engines[half],
+                        target.rearrange("p (s m u) -> p s m u", s=2, u=2),
+                        bank[:].rearrange("p (s u m) -> p s m u", s=2, u=2),
+                    )
 
-                jobs.append(([([("loaded", name)], fill)], work, None))
+                jobs.append(([([("loaded", name)], fill)], work, []))
             return jobs
 
-        def quantize_turned(name, operand):
-            return plain(lambda: quantize(operand[0][:], operand[1][:], live[name][:]), name)
+        def s_turn(g, engines):
+            return turn(("s", g), engines)
 
-        def w_group(q):
+        def p_turn(i, engine):
+            return turn(("p", i), [engine, engine])
+
+        def s_quantize(g):
+            return plain(lambda: quantize(s_mx[g][0][:], s_mx[g][1][:], live[("s", g)][:]), [("s", g)])
+
+        def p_quantize(i):
+            return plain(lambda: quantize(p_mx[i][0][:], p_mx[i][1][:], live[("p", i)][:]), [("p", i)])
+
+        def w_stage(q):
             def work():
-                target = staged_tile(("w", q))[:, : PACK * QUARTER].rearrange("p (c i j) -> p c j i", i=4, j=PACK)
-                source = raw[("w", q)][:].rearrange("p j (c i) -> p c j i", i=4)
+                target = staged_tile(("w", q))[:, : PACK * QUARTER].rearrange("p (c i j) -> p c j i", i=LINE, j=PACK)
+                source = raw[("w", q)][:].rearrange("p j (c i) -> p c j i", i=LINE)
                 nc.vector.tensor_scalar(out=target, in0=source, scalar1=-1.0, scalar2=None, op0=ALU.mult)
 
             return plain(work)
 
         def w_quantize(q):
-            return plain(lambda: quantize(w_mx[q][0][:], w_mx[q][1][:], live[("w", q)][:, : PACK * QUARTER]), ("w", q))
+            return plain(lambda: quantize(w_mx[q][0][:], w_mx[q][1][:], live[("w", q)][:, : PACK * QUARTER]), [("w", q)])
 
-        def fill_z(g, q, j):
+        def negate_scale():
+            nc.vector.tensor_scalar(out=neg_scale[:], in0=scale_raw[:], scalar1=-1.0, scalar2=None, op0=ALU.mult)
+
+        def later_loads(tiles, unit_groups):
+            def work():
+                for i in tiles:
+                    load_p(i)
+                for ug in unit_groups:
+                    nc.sync.dma_start(out=cap[ug][:], in_=cap_rows[ug])
+
+            return plain(work, [("loaded", ("p", i)) for i in tiles])
+
+        def z_passes(g, q, j):
             def fill(bank):
                 for t in range(PACK):
                     cols = slice(t * P, (t + 1) * P)
                     matmul(bank[:, cols], s_mx[g], cols, w_mx[q], slice(j * P, (j + 1) * P), True, True)
 
-            return fill
+            return [([("s", g), ("w", q)], fill)]
 
-        def block_of(g, q, j):
-            return live[("soft", g, q)][:, j * BANK : (j + 1) * BANK].rearrange("p (n t) -> p n t", t=PACK)
+        def soft_block(g, q, j):
+            return slots_last(live[("soft", g, q)][:, j * BANK : (j + 1) * BANK])
 
         def sigmoid_job(g, q, j):
             def work(bank):
                 if j == 0:
                     live[("soft", g, q)] = ringed("soft", 12, [P, PACK * QUARTER], F32)
-                nc.scalar.activation(out=block_of(g, q, j), in_=bank[:].rearrange("p (t n) -> p n t", t=PACK), func=ACT.Sigmoid)
+                nc.scalar.activation(out=soft_block(g, q, j), in_=bank_slots_last(bank), func=ACT.Sigmoid)
 
-            return ([([("s", g), ("w", q)], fill_z(g, q, j))], work, None)
+            return (z_passes(g, q, j), work, [])
 
-        def ln_job(g, q):
+        def sigmoids(pieces):
+            return [sigmoid_job(g, q, j) for (g, q) in pieces for j in range(BLOCKS)]
+
+        def ln_job(i):
             def work():
-                soft = live[("soft", g, q)]
+                soft = live[("soft",) + PIECES[i]]
                 nc.scalar.activation(out=soft[:], in_=soft[:], func=ACT.Ln, bias=LN_FLOOR)
 
             return plain(work)
 
-        def linear_job(g, q, j):
+        def linear_job(i, j):
+            g, q = PIECES[i]
+
             def work(bank):
                 nc.vector.scalar_tensor_tensor(
-                    out=block_of(g, q, j),
-                    in0=block_of(g, q, j),
+                    out=soft_block(g, q, j),
+                    in0=soft_block(g, q, j),
                     scalar=-LINEAR_FROM,
-                    in1=bank[:].rearrange("p (t n) -> p n t", t=PACK),
+                    in1=bank_slots_last(bank),
                     op0=ALU.max,
                     op1=ALU.min,
                 )
 
-            return ([([("s", g), ("w", q)], fill_z(g, q, j))], work, None)
+            return (z_passes(g, q, j), work, [])
 
-        def scale_job(g, q, blocks, on_gpsimd):
+        def staged_start(i):
+            return 0 if i % 2 == 0 else VECTOR_MANY
+
+        def scale_job(i, engine, low, high):
+            g, q = PIECES[i]
+            start = staged_start(i)
+
             def work():
-                width = P * len(blocks)
-                if on_gpsimd:
-                    staged = ringed("gpsimd_staged", 1, [P, PACK * width], BF16)
-                    engine = nc.gpsimd
-                else:
-                    staged = ringed("vector_staged", 2, [P, PACK * width], BF16)
-                    engine = nc.vector
-                live[("g", g, q, blocks)] = staged
-                source = live[("soft", g, q)][:, blocks[0] * BANK : (blocks[-1] + 1) * BANK]
                 engine.tensor_tensor(
-                    out=staged[:].rearrange("p (n t) -> p n t", t=PACK),
-                    in0=source.rearrange("p (n t) -> p n t", t=PACK),
-                    in1=neg_scale[:, g : g + 1, :].to_broadcast([P, width, PACK]),
+                    out=slots_last(g_staged[:, PACK * (start + low) : PACK * (start + high)]),
+                    in0=slots_last(live[("soft", g, q)][:, PACK * low : PACK * high]),
+                    in1=neg_scale[:, g : g + 1, :].to_broadcast([P, high - low, PACK]),
                     op=ALU.mult,
                 )
 
             return plain(work)
 
-        def g_quantize(g, q, blocks):
-            cols = slice(blocks[0] * P, (blocks[-1] + 1) * P)
-            codes, scales = g_mx[(g, q)]
-            gives = [("g", g, q, j) for j in blocks]
-            return plain(lambda: quantize(codes[:, cols], scales[:, cols], live[("g", g, q, blocks)][:]), gives)
+        def g_quantize(i):
+            codes, scales = g_mx[PIECES[i]]
+            start = staged_start(i)
+            staged = g_staged[:, PACK * start : PACK * (start + QUARTER)]
+            return plain(lambda: quantize(codes[:], scales[:], staged), [("g",) + PIECES[i]])
 
-        def shares(unit):
-            if unit == (3, 3):
-                return ((), (0, 1))
-            return ((0,), (1,)) if unit in HALVED else ((0, 1), ())
+        def step(i, psum_reads=(), quantises=()):
+            own = VECTOR_MANY if i + 1 in BARE_STEPS else VECTOR_FEW
+            if i % 2 == 0:
+                blocks, on_vector, on_gpsimd = (0, 1), (0, own), (own, QUARTER)
+            else:
+                blocks, on_vector, on_gpsimd = (1, 0), (QUARTER - own, QUARTER), (0, QUARTER - own)
+            first, second = [linear_job(i, j) for j in blocks]
+            if len(psum_reads) == PACK:
+                jobs = [first] + psum_reads[:2] + [second] + psum_reads[2:]
+            else:
+                jobs = [first, second] + list(psum_reads)
+            jobs = jobs + list(quantises) + [scale_job(i, nc.vector, *on_vector)]
+            if i > 0:
+                jobs = jobs + [g_quantize(i - 1)]
+            return jobs + [scale_job(i, nc.gpsimd, *on_gpsimd)]
 
-        def finish(unit):
-            on_gpsimd, on_vector = shares(unit)
-            return [g_quantize(*unit, blocks) for blocks in (on_vector, on_gpsimd) if blocks]
-
-        def g_step(previous, unit, psum_work=(), port_work=()):
-            on_gpsimd, on_vector = shares(unit)
-            step = [linear_job(*unit, 1), linear_job(*unit, 0)]
-            if psum_work:
-                step = weave(step, list(psum_work))
-            if on_vector:
-                step = step + [scale_job(*unit, on_vector, False)]
-            step = step + list(port_work)
-            if previous is not None:
-                step = step + finish(previous)
-            return step + ([scale_job(*unit, on_gpsimd, True)] if on_gpsimd else [])
-
-        def cap_job(ug, s, t):
-            first, width = SPANS[s]
-            quarters = range(first // QUARTER, (first + width) // QUARTER)
+        def cap_job(ug, q, t):
+            cols = slice(q * QUARTER, (q + 1) * QUARTER)
+            p_tile = PACK * ug + t
 
             def one_pass(g):
                 def fill(bank):
-                    matmul(bank[:, :width], p_mx[PACK * ug + t], slice(g * P, (g + 1) * P), g_mx[(g, s)], slice(0, width), g == 0, g == CELL_GROUPS - 1)
+                    m_cols = slice(g * P, (g + 1) * P)
+                    matmul(bank[:, :QUARTER], p_mx[p_tile], m_cols, g_mx[(g, q)], slice(0, QUARTER), g == 0, g == CELL_GROUPS - 1)
 
-                return ([("p", PACK * ug + t)] + [("g", g, q, j) for q in quarters for j in range(2)], fill)
+                return ([("p", p_tile), ("g", g, q)], fill)
 
             def work(bank):
                 if t == 0:
-                    live[("y", ug, s)] = ringed("y", 5, [P, PACK, width], F32)
-                y = live[("y", ug, s)]
+                    live[("y", ug, q)] = ringed("y", 5, [P, PACK, QUARTER], F32)
+                y = live[("y", ug, q)]
                 nc.vector.scalar_tensor_tensor(
                     out=y[:, t, :],
-                    in0=bank[:, :width],
+                    in0=bank[:, :QUARTER],
                     scalar=offset[:, ug, t : t + 1],
-                    in1=cap[ug][:, t, first : first + width],
+                    in1=cap[ug][:, t, cols],
                     op0=ALU.add,
                     op1=ALU.min,
                 )
                 if t == PACK - 1:
-                    nc.sync.dma_start(out=y_rows[ug][:, :, first : first + width], in_=y[:])
+                    nc.sync.dma_start(out=y_rows[ug][:, :, cols], in_=y[:])
 
-            return ([one_pass(g) for g in range(CELL_GROUPS)], work, None)
+            return ([one_pass(g) for g in range(CELL_GROUPS)], work, [])
 
-        def y_group(ug, s, engine="scalar"):
-            width = SPANS[s][1]
+        def caps(ug, q):
+            return [cap_job(ug, q, t) for t in range(PACK)]
 
+        def y_stage(ug, q, engine="scalar", low=0, high=QUARTER):
             def work():
-                target = staged_tile(("yb", ug, s))[:, : PACK * width].rearrange("p (c i t) -> p c t i", i=4, t=PACK)
-                source = live[("y", ug, s)][:].rearrange("p t (c i) -> p c t i", i=4)
-                if engine == "scalar":
-                    nc.scalar.copy(out=target, in_=source)
-                else:
-                    nc.vector.tensor_copy(out=target, in_=source)
+                target = staged_tile(("y_staged", ug, q))[:, PACK * low : PACK * high]
+                source = live[("y", ug, q)][:, :, low:high]
+                copy(
+                    engine,
+                    target.rearrange("p (c i t) -> p c t i", i=LINE, t=PACK),
+                    source.rearrange("p t (c i) -> p c t i", i=LINE),
+                )
 
             return plain(work)
 
-        def y_quantize(ug, s):
-            first, width = SPANS[s]
+        def y_quantize(ug, q):
+            cols = slice(q * QUARTER, (q + 1) * QUARTER)
 
             def work():
-                codes = ringed("y_codes", 3, [P, width], U32)
-                quantize(codes[:], y_scales[ug // 2][4 * (ug % 2) :, first : first + width], live[("yb", ug, s)][:, : PACK * width])
-                nc.sync.dma_start(out=words_out[ug][:, first : first + width], in_=codes[:].bitcast(I32))
-                if s == len(SPANS) - 1 and ug > 0:
-                    groups = slice(0, 2) if ug == 1 else slice(2, 3)
+                codes = ringed("y_codes", 3, [P, QUARTER], U32)
+                scales = y_scales[ug // 2]
+                quantize(codes[:], scales[4 * (ug % 2) :, cols], live[("y_staged", ug, q)][:, : PACK * QUARTER])
+                nc.sync.dma_start(out=words_out[ug][:, cols], in_=codes[:].bitcast(I32))
+                if q == QUARTERS - 1 and ug > 0:
+                    groups = slice(2 * (ug // 2), ug + 1)
                     rows = 4 * (groups.stop - groups.start)
                     for quad in range(4):
                         nc.sync.dma_start(
                             out=scales_out[groups, 4 * quad : 4 * quad + 4, :],
-                            in_=y_scales[ug // 2][32 * quad : 32 * quad + rows, :].bitcast(I32),
+                            in_=scales[32 * quad : 32 * quad + rows, :].bitcast(I32),
                         )
 
             return plain(work)
 
-        def negate_scale():
-            nc.vector.tensor_scalar(out=neg_scale[:], in0=scale_raw[:], scalar1=-1.0, scalar2=None, op0=ALU.mult)
+        first_banks = s_turn(0, ["scalar", "vector"])
+        order = first_banks[:1] + [w_stage(0)] + first_banks[1:] + [w_quantize(0), s_quantize(0), w_stage(1)]
+        order = order + s_turn(1, ["scalar", "vector"]) + [w_quantize(1), s_quantize(1)]
+        for g in (0, 1):
+            order = order + sigmoids([(g, 0)]) + s_turn(g + 2, ["vector", "vector"]) + sigmoids([(g, 1)])
+            order = order + [w_stage(g + 2), s_quantize(g + 2)]
+        order = order + [w_quantize(2), w_quantize(3), later_loads(range(4, 8), [0])]
+        order = order + sigmoids([(2, 0), (2, 1)]) + p_turn(0, "vector") + sigmoids([(3, 0)]) + p_turn(1, "vector") + [p_quantize(0)]
+        order = order + sigmoids([(3, 1)]) + p_turn(2, "vector") + [p_quantize(1), plain(negate_scale), p_quantize(2)]
+        order = order + [later_loads(range(8, P_TILES), [1, 2])] + p_turn(3, "vector")
 
-        def flat(steps):
-            return [job for step in steps for job in step]
+        second_sigmoids = sigmoids(PIECES[HALF:])
+        finished = [(ug, q) for q in range(QUARTERS) for ug in range(UNIT_GROUPS)]
+        order = order + [ln_job(0), ln_job(1)] + step(0)
+        for i in range(1, HALF - 1):
+            turned = p_turn(2 * i + 3, "vector") if 2 * i + 3 < P_TILES else []
+            jobs = step(i, turned, [p_quantize(p_tile) for p_tile in (2 * i + 1, 2 * i + 2) if p_tile < P_TILES])
+            if turned:
+                order = order + p_turn(2 * i + 2, "scalar")
+            if 2 * i < HALF:
+                order = order + [ln_job(2 * i), ln_job(2 * i + 1)] + jobs
+            else:
+                cut = i - HALF // 2
+                order = order + weave(second_sigmoids[SIGMOID_CUTS[cut] : SIGMOID_CUTS[cut + 1]], jobs)
+        order = order + step(HALF - 1, caps(*finished[0]))
 
-        def later_loads(names):
-            def work():
-                for name in names:
-                    if name[0] == "p":
-                        load_p(name[1])
-                    else:
-                        load_cap(name[1])
+        last = len(PIECES) - 1
+        order = order + [ln_job(HALF), ln_job(HALF + 1), y_stage(*finished[0])]
+        for i in range(HALF, last):
+            order = order + step(i, caps(*finished[i - HALF + 1]), [y_quantize(*finished[i - HALF])])
+            if i + 2 <= last:
+                order = order + [ln_job(i + 2)]
+            order = order + [y_stage(*finished[i - HALF + 1])]
 
-            return (None, work, [("loaded", name) for name in names])
+        order = order + weave([linear_job(last, 1), linear_job(last, 0)], caps(2, 2)) + [g_quantize(last - 1), y_quantize(1, 2)]
+        order = order + [scale_job(last, nc.vector, 0, QUARTER), y_stage(2, 2), y_quantize(2, 2), g_quantize(last)]
 
-        def p_copies(i, engine):
-            return turn_jobs(("p", i), [engine, engine])
+        order = order + caps(2, 3) + [y_stage(2, 3)] + caps(0, 3) + [y_stage(0, 3)]
+        order = order + caps(1, 3)[:2] + [y_quantize(2, 3)] + caps(1, 3)[2:] + [y_stage(1, 3, "scalar", 0, P), y_quantize(0, 3)]
+        order = order + [y_stage(1, 3, "vector", P, QUARTER), y_quantize(1, 3)]
 
-        def p_quantize(i):
-            return quantize_turned(("p", i), p_mx[i])
-
-        def epilogue(ug, s):
-            return [cap_job(ug, s, t) for t in range(PACK)]
-
-        cells = range(CELL_GROUPS)
-
-        def s_copies(g, engines):
-            return turn_jobs(("s", g), engines)
-
-        def s_quantize(g):
-            return quantize_turned(("s", g), s_mx[g])
-
-        def sigmoids(units):
-            return [sigmoid_job(g, q, j) for (g, q) in units for j in range(2)]
-
-        def quarter(q):
-            return [(g, q) for g in cells]
-
-        order = s_copies(0, ["scalar", "vector"])
-        order = order[:1] + [w_group(0)] + order[1:] + [w_quantize(0), s_quantize(0), w_group(1)]
-        order = order + s_copies(1, ["scalar", "vector"]) + [w_quantize(1), s_quantize(1)]
-        order = order + sigmoids([(0, 0)]) + s_copies(2, ["vector", "vector"]) + sigmoids([(0, 1)]) + [w_group(2), s_quantize(2)]
-        order = order + sigmoids([(1, 0)]) + s_copies(3, ["vector", "vector"]) + sigmoids([(1, 1)]) + [w_group(3), s_quantize(3), w_quantize(2), w_quantize(3)]
-        order = order + [later_loads([("p", 4), ("p", 5), ("p", 6), ("p", 7), ("cap", 0)])]
-        order = order + sigmoids([(2, 0), (2, 1)]) + p_copies(0, "vector") + sigmoids([(3, 0)]) + p_copies(1, "vector") + [p_quantize(0)]
-        order = order + sigmoids([(3, 1)]) + p_copies(2, "vector") + [p_quantize(1), plain(negate_scale), p_quantize(2)]
-        order = order + [later_loads([("p", 8), ("p", 9), ("p", 10), ("p", 11), ("cap", 1), ("cap", 2)])]
-        u = quarter(0) + quarter(1) + quarter(2) + quarter(3)
-        sig = sigmoids(quarter(2) + quarter(3))
-        order = order + [ln_job(*u[0]), ln_job(*u[1])] + g_step(None, u[0], p_copies(3, "vector"))
-        order = order + p_copies(4, "scalar") + [ln_job(*u[2]), ln_job(*u[3])] + g_step(u[0], u[1], p_copies(5, "vector"), [p_quantize(3), p_quantize(4)])
-        order = order + p_copies(6, "scalar") + [ln_job(*u[4]), ln_job(*u[5])] + g_step(u[1], u[2], p_copies(7, "vector"), [p_quantize(5), p_quantize(6)])
-        order = order + p_copies(8, "scalar") + [ln_job(*u[6]), ln_job(*u[7])] + g_step(u[2], u[3], p_copies(9, "vector"), [p_quantize(7)])
-        order = order + p_copies(10, "scalar") + weave(sig[:7], g_step(u[3], u[4], p_copies(11, "vector"), [p_quantize(8), p_quantize(9)]))
-        order = order + weave(sig[7:12], g_step(u[4], u[5], [], [p_quantize(10)]))
-        order = order + weave(sig[12:], g_step(u[5], u[6], [], [p_quantize(11)]))
-        order = order + g_step(u[6], u[7], epilogue(0, 0))
-        finished = [(ug, s) for s in range(4) for ug in range(UNIT_GROUPS)]
-        order = order + [ln_job(*u[8]), ln_job(*u[9]), y_group(0, 0)]
-        for i in range(8, 16):
-            order = order + g_step(u[i - 1], u[i], epilogue(*finished[i - 7]), [y_quantize(*finished[i - 8])])
-            if i + 2 < 16:
-                order = order + [ln_job(*u[i + 2])]
-            order = order + [y_group(*finished[i - 7])]
-        order = order + finish(u[15])
-        order = order + epilogue(0, 3) + [y_quantize(2, 2), y_group(0, 3)] + epilogue(1, 3) + [y_group(1, 3), y_quantize(0, 3)]
-        order = order + epilogue(2, 3)[:3] + [y_quantize(1, 3)] + epilogue(2, 3)[3:] + [y_group(2, 3, "vector"), y_quantize(2, 3)]
-
-        done = set(("loaded", name) for name in raw)
+        ready = set(("loaded", name) for name in list(raw) + [("s", 0)])
         banks = {}
         waiting = {}
         opened = 0
         for i, (passes, work, gives) in enumerate(order):
             while True:
                 for k in sorted(waiting):
-                    while waiting[k] and all(need in done for need in waiting[k][0][0]):
+                    while waiting[k] and all(need in ready for need in waiting[k][0][0]):
                         waiting[k][0][1](banks[k])
                         waiting[k] = waiting[k][1:]
                 if opened == len(order) or (opened > i and len(banks) >= BANKS_AHEAD):
                     break
                 ahead = order[opened][0]
                 if ahead is not None:
-                    if not all(need in done for need in ahead[0][0]):
+                    if not all(need in ready for need in ahead[0][0]):
                         break
                     banks[opened] = psum.tile([P, BANK], F32, name="bank", tag="bank")
                     waiting[opened] = list(ahead)
@@ -404,7 +432,4 @@ def tile_capped_evapotranspiration_planes_h3_kernel(
             else:
                 assert not waiting.pop(i)
                 work(banks.pop(i))
-            if isinstance(gives, list):
-                done = done | set(gives)
-            elif gives is not None:
-                done.add(gives)
+            ready = ready | set(gives)

from contextlib import ExitStack

import concourse.mybir as mybir
from concourse.masks import make_identity

C, K, F, U = 2048, 512, 1024, 1536
FLOPS = 2 * C * K * F + 2 * U * C * F

F32 = mybir.dt.float32
BF16 = mybir.dt.bfloat16
I32 = mybir.dt.int32
U32 = mybir.dt.uint32
U8 = mybir.dt.uint8
FP8X4 = mybir.dt.float8_e4m3fn_x4
ALU = mybir.AluOpType
ACT = mybir.ActivationFunctionType

P = 128
PACK = 4
PASS = P * PACK
BANK = 512
ROW_WORDS = PASS // 2
CELL_GROUPS = C // PASS
UNIT_GROUPS = U // PASS
P_TILES = U // P
QUARTER = 256
QUARTERS = F // QUARTER
BLOCKS = QUARTER // P
LINE = 4

LINEAR_FROM = 20.0
LN_FLOOR = 2.0**-60

PIECES = [(g, q) for q in range(QUARTERS) for g in range(CELL_GROUPS)]
HALF = len(PIECES) // 2

VECTOR_FEW = 56
VECTOR_MANY = 160
BARE_STEPS = (5, 6)
SIGMOID_CUTS = (0, 7, 12, BLOCKS * HALF)
BANKS_AHEAD = 6


def weave(first, second):
    keyed = [((i + 0.5) / len(first), 0, i, job) for i, job in enumerate(first)]
    keyed = keyed + [((i + 0.5) / len(second), 1, i, job) for i, job in enumerate(second)]
    return [entry[3] for entry in sorted(keyed, key=lambda entry: entry[:3])]


def tile_capped_evapotranspiration_planes_h3_kernel(
    tc, soil_states, feature_weights, cell_scale, et_weights, et_offset, et_cap, out_0, out_1, out_2
):
    nc = tc.nc
    with ExitStack() as ctx:
        keep = ctx.enter_context(tc.tile_pool(name="keep", bufs=1))
        ring = ctx.enter_context(tc.tile_pool(name="ring", bufs=1))
        psum = ctx.enter_context(tc.psum_pool(name="psum", bufs=8))
        ctx.enter_context(tc.manual_schedule())

        def kept(name, shape, dtype):
            return keep.tile(shape, dtype, name=name, align_bytes=64)

        def ringed(tag, bufs, shape, dtype):
            return ring.tile(shape, dtype, name=tag, tag=tag, bufs=bufs, align_bytes=64)

        def mx_operand(name, width):
            return kept(name + "_codes", [P, width], U32), kept(name + "_scales", [P, width], U8)

        def quantize(codes, scales, staged):
            nc.vector.quantize_mx(out=codes.bitcast(FP8X4), scales=scales, in_=staged)

        def matmul(out, stationary, m_cols, moving, n_cols, start, stop):
            nc.tensor.matmul_mx(
                out=out,
                lhsT=stationary[0][:, m_cols].bitcast(FP8X4),
                lhsT_scale=stationary[1][:, m_cols],
                rhs=moving[0][:, n_cols].bitcast(FP8X4),
                rhs_scale=moving[1][:, n_cols],
                start=start,
                stop=stop,
            )

        def copy(engine, out, in_):
            if engine == "scalar":
                nc.scalar.copy(out=out, in_=in_)
            else:
                nc.vector.tensor_copy(out=out, in_=in_)

        def slots_last(ap):
            return ap.rearrange("p (n t) -> p n t", t=PACK)

        def bank_slots_last(bank):
            return bank[:].rearrange("p (t n) -> p n t", t=PACK)

        identity = kept("identity", [P, P], F32)
        make_identity(nc, identity[:])

        s_rows = soil_states.rearrange("(g m t) k -> g m (t k)", m=P, t=PACK)
        w_rows = feature_weights.rearrange("(p j) n -> p j n", j=PACK)
        p_rows = et_weights.rearrange("(g m t) c -> g t m c", m=P, t=PACK)
        cap_rows = et_cap.rearrange("(g m t) n -> g m t n", m=P, t=PACK)
        y_rows = out_0.rearrange("(g m t) n -> g m t n", m=P, t=PACK)
        words_out = out_1.rearrange("g p n t -> g p (n t)").bitcast(I32)
        scales_out = out_2.bitcast(I32)

        raw = {}
        first_halves = []

        def load_raw(name, source):
            raw[name] = ringed("raw", 11, list(source.shape), BF16)
            nc.sync.dma_start(out=raw[name][:], in_=source)

        def load_first_half(half):
            rows = ringed("raw_half", 2, [P, 2 * K], BF16)
            nc.sync.dma_start(out=rows[:], in_=s_rows[0][:, half * 2 * K : (half + 1) * 2 * K])
            first_halves.append(rows)

        def load_s(g):
            load_raw(("s", g), s_rows[g])

        def load_w(q):
            load_raw(("w", q), w_rows[:, :, q * QUARTER : (q + 1) * QUARTER])

        def load_p(i):
            load_raw(("p", i), p_rows[i // PACK, i % PACK])

        load_first_half(0)
        load_w(0)
        load_first_half(1)
        load_s(1)
        load_w(1)
        load_s(2)
        load_w(2)
        load_s(3)
        load_w(3)
        load_p(0)
        load_p(1)
        scale_raw = kept("scale_raw", [P, CELL_GROUPS, PACK], BF16)
        nc.sync.dma_start(out=scale_raw[:], in_=cell_scale.rearrange("(g p t) -> p g t", p=P, t=PACK))
        load_p(2)
        load_p(3)
        offset = kept("offset", [P, UNIT_GROUPS, PACK], BF16)
        nc.sync.dma_start(out=offset[:], in_=et_offset.rearrange("(g p t) -> p g t", p=P, t=PACK))

        cap = [kept("cap%d" % ug, [P, PACK, F], BF16) for ug in range(UNIT_GROUPS)]
        s_mx = [mx_operand("s%d" % g, PASS) for g in range(CELL_GROUPS)]
        w_mx = [mx_operand("w%d" % q, QUARTER) for q in range(QUARTERS)]
        p_mx = [mx_operand("p%d" % i, PASS) for i in range(P_TILES)]
        g_mx = {(g, q): mx_operand("g%d_%d" % (g, q), QUARTER) for g in range(CELL_GROUPS) for q in range(QUARTERS)}
        y_scales = [kept("y_scales%d" % pair, [P, F], U8) for pair in range(2)]
        neg_scale = kept("neg_scale", [P, CELL_GROUPS, PACK], F32)
        g_staged = kept("g_staged", [P, PACK * (QUARTER + VECTOR_MANY)], BF16)

        live = {}

        def plain(work, gives=()):
            return (None, work, list(gives))

        def staged_tile(key):
            if key not in live:
                live[key] = ringed("staged", 5, [P, PACK * PASS], BF16)
            return live[key]

        def turn(name, engines):
            jobs = []
            for half in range(2):

                def fill(bank, half=half):
                    if name == ("s", 0):
                        words = first_halves[half][:].bitcast(F32)
                    else:
                        words = raw[name][:].bitcast(F32)[:, half * BANK : (half + 1) * BANK]
                    for part in range(2):
                        for u in range(2):
                            col = (2 * part + u) * P
                            source = words[:, part * ROW_WORDS + u : (part + 1) * ROW_WORDS : 2]
                            nc.tensor.transpose(bank[:, col : col + P], source, identity[:])

                def work(bank, half=half):
                    target = staged_tile(name)[:].bitcast(F32)[:, half * BANK : (half + 1) * BANK]
                    copy(
                        engines[half],
                        target.rearrange("p (s m u) -> p s m u", s=2, u=2),
                        bank[:].rearrange("p (s u m) -> p s m u", s=2, u=2),
                    )

                jobs.append(([([("loaded", name)], fill)], work, []))
            return jobs

        def s_turn(g, engines):
            return turn(("s", g), engines)

        def p_turn(i, engine):
            return turn(("p", i), [engine, engine])

        def s_quantize(g):
            return plain(lambda: quantize(s_mx[g][0][:], s_mx[g][1][:], live[("s", g)][:]), [("s", g)])

        def p_quantize(i):
            return plain(lambda: quantize(p_mx[i][0][:], p_mx[i][1][:], live[("p", i)][:]), [("p", i)])

        def w_stage(q):
            def work():
                target = staged_tile(("w", q))[:, : PACK * QUARTER].rearrange("p (c i j) -> p c j i", i=LINE, j=PACK)
                source = raw[("w", q)][:].rearrange("p j (c i) -> p c j i", i=LINE)
                nc.vector.tensor_scalar(out=target, in0=source, scalar1=-1.0, scalar2=None, op0=ALU.mult)

            return plain(work)

        def w_quantize(q):
            return plain(lambda: quantize(w_mx[q][0][:], w_mx[q][1][:], live[("w", q)][:, : PACK * QUARTER]), [("w", q)])

        def negate_scale():
            nc.vector.tensor_scalar(out=neg_scale[:], in0=scale_raw[:], scalar1=-1.0, scalar2=None, op0=ALU.mult)

        def later_loads(tiles, unit_groups):
            def work():
                for i in tiles:
                    load_p(i)
                for ug in unit_groups:
                    nc.sync.dma_start(out=cap[ug][:], in_=cap_rows[ug])

            return plain(work, [("loaded", ("p", i)) for i in tiles])

        def z_passes(g, q, j):
            def fill(bank):
                for t in range(PACK):
                    cols = slice(t * P, (t + 1) * P)
                    matmul(bank[:, cols], s_mx[g], cols, w_mx[q], slice(j * P, (j + 1) * P), True, True)

            return [([("s", g), ("w", q)], fill)]

        def soft_block(g, q, j):
            return slots_last(live[("soft", g, q)][:, j * BANK : (j + 1) * BANK])

        def sigmoid_job(g, q, j):
            def work(bank):
                if j == 0:
                    live[("soft", g, q)] = ringed("soft", 12, [P, PACK * QUARTER], F32)
                nc.scalar.activation(out=soft_block(g, q, j), in_=bank_slots_last(bank), func=ACT.Sigmoid)

            return (z_passes(g, q, j), work, [])

        def sigmoids(pieces):
            return [sigmoid_job(g, q, j) for (g, q) in pieces for j in range(BLOCKS)]

        def ln_job(i):
            def work():
                soft = live[("soft",) + PIECES[i]]
                nc.scalar.activation(out=soft[:], in_=soft[:], func=ACT.Ln, bias=LN_FLOOR)

            return plain(work)

        def linear_job(i, j):
            g, q = PIECES[i]

            def work(bank):
                nc.vector.scalar_tensor_tensor(
                    out=soft_block(g, q, j),
                    in0=soft_block(g, q, j),
                    scalar=-LINEAR_FROM,
                    in1=bank_slots_last(bank),
                    op0=ALU.max,
                    op1=ALU.min,
                )

            return (z_passes(g, q, j), work, [])

        def staged_start(i):
            return 0 if i % 2 == 0 else VECTOR_MANY

        def scale_job(i, engine, low, high):
            g, q = PIECES[i]
            start = staged_start(i)

            def work():
                engine.tensor_tensor(
                    out=slots_last(g_staged[:, PACK * (start + low) : PACK * (start + high)]),
                    in0=slots_last(live[("soft", g, q)][:, PACK * low : PACK * high]),
                    in1=neg_scale[:, g : g + 1, :].to_broadcast([P, high - low, PACK]),
                    op=ALU.mult,
                )

            return plain(work)

        def g_quantize(i):
            codes, scales = g_mx[PIECES[i]]
            start = staged_start(i)
            staged = g_staged[:, PACK * start : PACK * (start + QUARTER)]
            return plain(lambda: quantize(codes[:], scales[:], staged), [("g",) + PIECES[i]])

        def step(i, psum_reads=(), quantises=()):
            own = VECTOR_MANY if i + 1 in BARE_STEPS else VECTOR_FEW
            if i % 2 == 0:
                blocks, on_vector, on_gpsimd = (0, 1), (0, own), (own, QUARTER)
            else:
                blocks, on_vector, on_gpsimd = (1, 0), (QUARTER - own, QUARTER), (0, QUARTER - own)
            first, second = [linear_job(i, j) for j in blocks]
            if len(psum_reads) == PACK:
                jobs = [first] + psum_reads[:2] + [second] + psum_reads[2:]
            else:
                jobs = [first, second] + list(psum_reads)
            jobs = jobs + list(quantises) + [scale_job(i, nc.vector, *on_vector)]
            if i > 0:
                jobs = jobs + [g_quantize(i - 1)]
            return jobs + [scale_job(i, nc.gpsimd, *on_gpsimd)]

        def cap_job(ug, q, t):
            cols = slice(q * QUARTER, (q + 1) * QUARTER)
            p_tile = PACK * ug + t

            def one_pass(g):
                def fill(bank):
                    m_cols = slice(g * P, (g + 1) * P)
                    matmul(bank[:, :QUARTER], p_mx[p_tile], m_cols, g_mx[(g, q)], slice(0, QUARTER), g == 0, g == CELL_GROUPS - 1)

                return ([("p", p_tile), ("g", g, q)], fill)

            def work(bank):
                if t == 0:
                    live[("y", ug, q)] = ringed("y", 5, [P, PACK, QUARTER], F32)
                y = live[("y", ug, q)]
                nc.vector.scalar_tensor_tensor(
                    out=y[:, t, :],
                    in0=bank[:, :QUARTER],
                    scalar=offset[:, ug, t : t + 1],
                    in1=cap[ug][:, t, cols],
                    op0=ALU.add,
                    op1=ALU.min,
                )
                if t == PACK - 1:
                    nc.sync.dma_start(out=y_rows[ug][:, :, cols], in_=y[:])

            return ([one_pass(g) for g in range(CELL_GROUPS)], work, [])

        def caps(ug, q):
            return [cap_job(ug, q, t) for t in range(PACK)]

        def y_stage(ug, q, engine="scalar", low=0, high=QUARTER):
            def work():
                target = staged_tile(("y_staged", ug, q))[:, PACK * low : PACK * high]
                source = live[("y", ug, q)][:, :, low:high]
                copy(
                    engine,
                    target.rearrange("p (c i t) -> p c t i", i=LINE, t=PACK),
                    source.rearrange("p t (c i) -> p c t i", i=LINE),
                )

            return plain(work)

        def y_quantize(ug, q):
            cols = slice(q * QUARTER, (q + 1) * QUARTER)

            def work():
                codes = ringed("y_codes", 3, [P, QUARTER], U32)
                scales = y_scales[ug // 2]
                quantize(codes[:], scales[4 * (ug % 2) :, cols], live[("y_staged", ug, q)][:, : PACK * QUARTER])
                nc.sync.dma_start(out=words_out[ug][:, cols], in_=codes[:].bitcast(I32))
                if q == QUARTERS - 1 and ug > 0:
                    groups = slice(2 * (ug // 2), ug + 1)
                    rows = 4 * (groups.stop - groups.start)
                    for quad in range(4):
                        nc.sync.dma_start(
                            out=scales_out[groups, 4 * quad : 4 * quad + 4, :],
                            in_=scales[32 * quad : 32 * quad + rows, :].bitcast(I32),
                        )

            return plain(work)

        first_banks = s_turn(0, ["scalar", "vector"])
        order = first_banks[:1] + [w_stage(0)] + first_banks[1:] + [w_quantize(0), s_quantize(0), w_stage(1)]
        order = order + s_turn(1, ["scalar", "vector"]) + [w_quantize(1), s_quantize(1)]
        for g in (0, 1):
            order = order + sigmoids([(g, 0)]) + s_turn(g + 2, ["vector", "vector"]) + sigmoids([(g, 1)])
            order = order + [w_stage(g + 2), s_quantize(g + 2)]
        order = order + [w_quantize(2), w_quantize(3), later_loads(range(4, 8), [0])]
        order = order + sigmoids([(2, 0), (2, 1)]) + p_turn(0, "vector") + sigmoids([(3, 0)]) + p_turn(1, "vector") + [p_quantize(0)]
        order = order + sigmoids([(3, 1)]) + p_turn(2, "vector") + [p_quantize(1), plain(negate_scale), p_quantize(2)]
        order = order + [later_loads(range(8, P_TILES), [1, 2])] + p_turn(3, "vector")

        second_sigmoids = sigmoids(PIECES[HALF:])
        finished = [(ug, q) for q in range(QUARTERS) for ug in range(UNIT_GROUPS)]
        order = order + [ln_job(0), ln_job(1)] + step(0)
        for i in range(1, HALF - 1):
            turned = p_turn(2 * i + 3, "vector") if 2 * i + 3 < P_TILES else []
            jobs = step(i, turned, [p_quantize(p_tile) for p_tile in (2 * i + 1, 2 * i + 2) if p_tile < P_TILES])
            if turned:
                order = order + p_turn(2 * i + 2, "scalar")
            if 2 * i < HALF:
                order = order + [ln_job(2 * i), ln_job(2 * i + 1)] + jobs
            else:
                cut = i - HALF // 2
                order = order + weave(second_sigmoids[SIGMOID_CUTS[cut] : SIGMOID_CUTS[cut + 1]], jobs)
        order = order + step(HALF - 1, caps(*finished[0]))

        last = len(PIECES) - 1
        order = order + [ln_job(HALF), ln_job(HALF + 1), y_stage(*finished[0])]
        for i in range(HALF, last):
            order = order + step(i, caps(*finished[i - HALF + 1]), [y_quantize(*finished[i - HALF])])
            if i + 2 <= last:
                order = order + [ln_job(i + 2)]
            order = order + [y_stage(*finished[i - HALF + 1])]

        order = order + weave([linear_job(last, 1), linear_job(last, 0)], caps(2, 2)) + [g_quantize(last - 1), y_quantize(1, 2)]
        order = order + [scale_job(last, nc.vector, 0, QUARTER), y_stage(2, 2), y_quantize(2, 2), g_quantize(last)]

        order = order + caps(2, 3) + [y_stage(2, 3)] + caps(0, 3) + [y_stage(0, 3)]
        order = order + caps(1, 3)[:2] + [y_quantize(2, 3)] + caps(1, 3)[2:] + [y_stage(1, 3, "scalar", 0, P), y_quantize(0, 3)]
        order = order + [y_stage(1, 3, "vector", P, QUARTER), y_quantize(1, 3)]

        ready = set(("loaded", name) for name in list(raw) + [("s", 0)])
        banks = {}
        waiting = {}
        opened = 0
        for i, (passes, work, gives) in enumerate(order):
            while True:
                for k in sorted(waiting):
                    while waiting[k] and all(need in ready for need in waiting[k][0][0]):
                        waiting[k][0][1](banks[k])
                        waiting[k] = waiting[k][1:]
                if opened == len(order) or (opened > i and len(banks) >= BANKS_AHEAD):
                    break
                ahead = order[opened][0]
                if ahead is not None:
                    if not all(need in ready for need in ahead[0][0]):
                        break
                    banks[opened] = psum.tile([P, BANK], F32, name="bank", tag="bank")
                    waiting[opened] = list(ahead)
                opened = opened + 1
            if passes is None:
                work()
            else:
                assert not waiting.pop(i)
                work(banks.pop(i))
            ready = ready | set(gives)
